import numpy as np
import ml_dtypes


def mxq(x, axis, fmt="e4m3"):
    dtype, down = {"e4m3": (ml_dtypes.float8_e4m3fn, 7), "e5m2": (ml_dtypes.float8_e5m2, 14)}[fmt]
    v = np.moveaxis(np.asarray(x, np.float32).astype(ml_dtypes.bfloat16).astype(np.float64), axis, -1)
    blocks = v.reshape(v.shape[:-1] + (-1, 32))
    amax = np.abs(blocks).max(-1, keepdims=True)
    byte = np.maximum(np.where(amax > 0, np.frexp(amax)[1] - 1 + 127, 0) - down, 1)
    scale = np.exp2(byte - 127.0)
    codes = (blocks / scale).astype(np.float32).astype(dtype).astype(np.float64)
    return np.moveaxis((codes * scale).reshape(v.shape), -1, axis)


WIDE = False


def mx_kscale(k):
    if not WIDE:
        return np.ones(k)
    levels = np.array([10, -10, 5, -5, 0])
    if k % 512:
        return np.exp2(np.random.permutation(np.resize(levels, k // 32))).repeat(32)
    a = np.empty((k // 512, 16))
    for p in range(k // 512):
        a[p, :8] = np.random.permutation(np.resize(levels, 8))
        for g in range(8):
            far = levels[np.abs(levels - a[p, g]) >= 10]
            a[p, g + 8] = far[np.random.randint(len(far))]
    return np.exp2(a.ravel()).repeat(32)


def f64(x):
    return np.asarray(x).astype(np.float64)


def striped(idx):
    return np.tile(idx.reshape(-1, 16).T, (8, 1)).astype(np.uint16)


def unstriped(offs):
    return offs[:16].T.reshape(-1).astype(np.int64)


def striped8(idx):
    return np.concatenate([x.reshape(-1, 16).T for x in idx]).astype(np.uint16)


def runs(offs, k):
    lists = np.stack([offs[16 * r : 16 * r + 16].T.reshape(-1) for r in range(8)]).astype(np.int64)
    return lists[np.arange(k) % 512 // 64]


def pack_weight(w):
    k, n = w.shape
    w = f64(np.asarray(w, np.float32).astype(ml_dtypes.bfloat16)).reshape(k // 32, 32, n)
    amax = np.abs(w).max(1)
    byte = np.clip(np.where(amax > 0, np.frexp(amax)[1] - 1 + 127 - 7, 1), 1, 254)
    scaled = (w * np.exp2(127.0 - byte)[:, None, :]).reshape(k, n).astype(np.float32)
    words = np.ascontiguousarray(scaled.reshape(k // 512, 128, 4, n).transpose(0, 1, 3, 2)).astype(ml_dtypes.float8_e4m3fn).view(np.uint8)
    return words, np.ascontiguousarray(byte.astype(np.uint8).reshape(k // 512, 16, n))


def unpack_weight(words, scales):
    g, p, n, _ = words.shape
    vals = np.ascontiguousarray(words).view(ml_dtypes.float8_e4m3fn).astype(np.float64) * np.repeat(np.exp2(scales.astype(np.float64) - 127.0), 8, axis=1)[..., None]
    return vals.transpose(0, 1, 3, 2).reshape(g * 512, n)


def sigmoid(v):
    return 1.0 / (1.0 + np.exp(-np.maximum(v, -700.0)))

def planes(y):
    n, m = y.shape
    v = y.astype(np.float32).astype(ml_dtypes.bfloat16).astype(np.float64).reshape(n // 32, 32, m)
    top = np.abs(v).max(1)
    byte = np.clip(np.where(top > 0, np.frexp(top)[1] - 1 + 127 - 7, 1), 1, 254)
    codes = (v * np.exp2(127.0 - byte)[:, None, :]).reshape(n, m).astype(np.float32).astype(ml_dtypes.float8_e4m3fn).view(np.uint8)
    words = codes.reshape(n // 512, 128, 4, m).transpose(0, 1, 3, 2)
    return np.ascontiguousarray(words), np.ascontiguousarray(byte.astype(np.uint8).reshape(n // 512, 16, m))


K, T, S, V, G, H = 512, 2048, 1024, 512, 2048, 512


def setup_inputs():
    n = np.random.standard_normal
    s = mx_kscale(K)[:, None]
    packed_xT = pack_weight(n((K, T)) * s)
    packed_dT = pack_weight(n((K, G)) / s)
    return {
        "x_words": packed_xT[0],
        "x_scales": packed_xT[1],
        "d_words": packed_dT[0],
        "d_scales": packed_dT[1],
        "gs": (np.random.uniform(0.5, 1.5, (K, 1)) * s).astype(np.float32),
        "offs": striped(np.random.permutation(T)[:S]),
        "k1": striped8(np.random.randint(0, G, (8, H))),
        "n1": striped8(np.stack([np.random.permutation(S) for _ in range(8)])),
        "n2": striped8(np.stack([np.random.permutation(V) for _ in range(8)])),
        "n3": striped8(np.stack([np.random.permutation(V) for _ in range(8)])),
    }


def reference(x_words, x_scales, d_words, d_scales, gs, offs, k1, n1, n2, n3):
    d_k1 = unpack_weight(d_words, d_scales)[np.arange(K)[:, None], runs(k1, K)]
    xq = unpack_weight(x_words, x_scales)[:, unstriped(offs)]
    h = 0.0625 * (d_k1.T @ xq)
    ln = h[np.arange(H)[:, None], runs(n1, H)]
    mx = ln.reshape(H, V, 2).max(axis=2)
    mn = ln.reshape(H, V, 2).min(axis=2)
    z = f64(gs) * (mx - (0.5 * mn))
    h2 = 0.0625 * ((d_k1.T @ mxq(z, 0, "e4m3")))
    out_0 = h2 + (sigmoid(h2[np.arange(H)[:, None], runs(n2, H)])) * (h2[np.arange(H)[:, None], runs(n3, H)] - h2)
    return (out_0,) + planes(out_0)

@@ -1,0 +1,182 @@
+from contextlib import ExitStack
+
+import concourse.mybir as mybir
+
+F32 = mybir.dt.float32
+BF16 = mybir.dt.bfloat16
+I32 = mybir.dt.int32
+U32 = mybir.dt.uint32
+U16 = mybir.dt.uint16
+U8 = mybir.dt.uint8
+FP8X4 = mybir.dt.float8_e4m3fn_x4
+ALU = mybir.AluOpType
+ACT = mybir.ActivationFunctionType
+
+P = 128
+PACK = 4
+T, S, V, G, H = 2048, 1024, 512, 2048, 512
+FLOPS = 2 * 512 * H * (S + V)
+Z_CHUNKS = [256,128,128]
+OUT_CHUNKS = [256,128,128]
+
+
+def spans(widths):
+    starts = [sum(widths[:i]) for i in range(len(widths))]
+    return list(zip(starts, widths))
+
+
+def tile_picked_ringpgaptrack_none_po_kernel(
+    tc, x_words, x_scales, d_words, d_scales, gs, offs, k1, n1, n2, n3, out_0, out_1, out_2
+):
+    nc = tc.nc
+    with ExitStack() as ctx:
+        keep = ctx.enter_context(tc.tile_pool(name="keep", bufs=1))
+        psum = ctx.enter_context(tc.psum_pool(name="psum", bufs=1))
+
+        def sb(shape, dtype, name):
+            return keep.tile(shape, dtype, name=name, align_bytes=64)
+
+        offs_sb = sb([P, S // 16], U16, "offs_sb")
+        k1_sb = sb([P, H // 16], U16, "k1_sb")
+        n1_sb = sb([P, S // 16], U16, "n1_sb")
+        n2_sb = sb([P, V // 16], U16, "n2_sb")
+        n3_sb = sb([P, V // 16], U16, "n3_sb")
+        xw_all = sb([P, T], I32, "xw_all")
+        dw_all = sb([P, G], I32, "dw_all")
+        xs_all = sb([P, T], U8, "xs_all")
+        ds_all = sb([P, G], U8, "ds_all")
+        ds_plane = sb([P, H], U8, "ds_plane")
+        gs_sb = sb([P, PACK], F32, "gs_sb")
+
+        nc.vector.memset(ds_all[:].bitcast(I32), 0)
+        nc.vector.memset(xs_all[:].bitcast(I32), 0)
+        nc.vector.memset(ds_plane[:].bitcast(I32), 0)
+
+        nc.sync.dma_start(k1_sb[:], k1)
+        nc.sync.dma_start(offs_sb[:], offs)
+        nc.sync.dma_start(n1_sb[:], n1)
+        nc.scalar.dma_start(ds_all[0:P:8, :].bitcast(I32), d_scales[0].bitcast(I32))
+        nc.sync.dma_start(dw_all[:], d_words[0].rearrange("p n j -> p (n j)").bitcast(I32))
+        nc.sync.dma_start(xw_all[:], x_words[0].rearrange("p n j -> p (n j)").bitcast(I32))
+        nc.sync.dma_start(n2_sb[:], n2)
+        nc.sync.dma_start(n3_sb[:], n3)
+        for q in range(4):
+            nc.gpsimd.dma_start(xs_all[32 * q : 32 * q + 4, :].bitcast(I32), x_scales[0][4 * q : 4 * q + 4, :].bitcast(I32))
+        nc.gpsimd.dma_start(gs_sb[:], gs.rearrange("(p t) o -> p (t o)", t=PACK))
+
+        warm = sb([P, 1], F32, "warm")
+        nc.gpsimd.memset(warm[:], 0.0)
+        nc.scalar.activation(warm[:], warm[:], ACT.Sigmoid)
+
+        gs_64th = sb([P, PACK], F32, "gs_64th")
+        gs_sign = sb([P, PACK], F32, "gs_sign")
+        nc.scalar.activation(gs_64th[:], gs_sb[:], ACT.Copy, scale=1.0 / 64.0)
+        nc.scalar.activation(gs_sign[:], gs_sb[:], ACT.Sign)
+
+        ds_picked = sb([P, H], U8, "ds_picked")
+        ds_dealt = sb([P, H], U8, "ds_dealt")
+        nc.vector.tensor_copy(ds_picked[:], ds_all[:].indirect(k1_sb[:]))
+        nc.vector.tensor_copy(
+            ds_dealt[:].rearrange("p (t m) -> p t m", t=PACK), ds_picked[:].rearrange("p (m t) -> p t m", t=PACK)
+        )
+        for q in range(4):
+            nc.sync.dma_start(
+                ds_plane[32 * q : 32 * q + 4, :].bitcast(I32), ds_dealt[32 * q : 32 * q + 32 : 8, :].bitcast(I32)
+            )
+
+        half = S // 2
+        xs = [sb([P, half], U8, f"xs{u}") for u in range(2)]
+        xw = [sb([P, half], U32, f"xw{u}") for u in range(2)]
+        half_lists = [offs_sb[:, u * half // 16 : (u + 1) * half // 16] for u in range(2)]
+        nc.vector.tensor_copy(xs[0][:], xs_all[:].indirect(half_lists[0]))
+
+        dw_picked = sb([P, H], U32, "dw_picked")
+        dw_dealt = sb([P, H], U32, "dw_dealt")
+        nc.vector.tensor_copy(dw_picked[:], dw_all[:].bitcast(U32).indirect(k1_sb[:]))
+        nc.vector.tensor_copy(
+            dw_dealt[:].rearrange("p (t m) -> p t m", t=PACK), dw_picked[:].rearrange("p (m t) -> p t m", t=PACK)
+        )
+        nc.vector.tensor_copy(xs[1][:], xs_all[:].indirect(half_lists[1]))
+
+        def product(bank, t, words, scales):
+            cols = slice(t * P, (t + 1) * P)
+            nc.tensor.matmul_mx(
+                out=bank,
+                lhsT=dw_dealt[:, cols].bitcast(FP8X4),
+                lhsT_scale=ds_plane[:, cols],
+                rhs=words.bitcast(FP8X4),
+                rhs_scale=scales,
+                start=True,
+                stop=True,
+            )
+
+        h = [sb([P, S], F32, f"h{t}") for t in range(PACK)]
+        h_banks = {}
+        for u in range(2):
+            nc.vector.tensor_copy(xw[u][:], xw_all[:].bitcast(U32).indirect(half_lists[u]))
+            for t in range(PACK):
+                h_banks[t, u] = psum.tile([P, half], F32, name=f"h_bank{t}{u}", tag=f"bank{PACK * u + t}")
+                product(h_banks[t, u][:], t, xw[u][:], xs[u][:])
+        for t, u in [(t, u) for t in range(PACK) for u in range(2)]:
+            nc.scalar.activation(
+                h[t][:, u * half : (u + 1) * half], h_banks[t, u][:], ACT.Copy, scale=gs_64th[:, t : t + 1]
+            )
+
+        h2 = [sb([P, V], F32, f"h2{t}") for t in range(PACK)]
+        h2_again = sb([P, PACK, V], F32, "h2_again")
+        for c, (v0, w) in enumerate(spans(Z_CHUNKS)):
+            lined = sb([P, PACK, 2 * w], F32, f"lined{c}")
+            for t in range(PACK):
+                nc.vector.tensor_copy(lined[:, t, :], h[t][:].indirect(n1_sb[:, 2 * v0 // 16 : 2 * (v0 + w) // 16]))
+            pairs = lined[:].rearrange("p t (v e) -> p (t v) e", e=2)
+            gap = sb([P, PACK * w], F32, f"gap{c}")
+            total = sb([P, PACK * w], F32, f"total{c}")
+            nc.vector.tensor_tensor(gap[:], pairs[:, :, 0], pairs[:, :, 1], ALU.subtract)
+            nc.vector.tensor_tensor(total[:], pairs[:, :, 0], pairs[:, :, 1], ALU.add)
+            spread = sb([P, PACK * w], F32, f"spread{c}")
+            nc.scalar.activation(spread[:], gap[:], ACT.Abs, scale=3.0)
+            z = sb([P, PACK * w], F32, f"z{c}")
+            for t in range(PACK):
+                row = slice(t * w, (t + 1) * w)
+                nc.vector.scalar_tensor_tensor(
+                    z[:, row], spread[:, row], gs_sign[:, t : t + 1], total[:, row], ALU.mult, ALU.add
+                )
+            z_bf = sb([P, PACK * w], BF16, f"z_bf{c}")
+            nc.scalar.copy(z_bf[:].rearrange("p (v t) -> p v t", t=PACK), z[:].rearrange("p (t v) -> p v t", t=PACK))
+            z_words = sb([P, w], U32, f"z_words{c}")
+            z_scales = sb([P, w], U8, f"z_scales{c}")
+            nc.vector.quantize_mx(out=z_words[:].bitcast(FP8X4), scales=z_scales[:], in_=z_bf[:])
+            banks = []
+            for t in range(PACK):
+                bank = psum.tile([P, w], F32, name=f"h2_bank{c}{t}", tag=f"bank{PACK * (c % 2) + t}")
+                product(bank[:], t, z_words[:], z_scales[:])
+                nc.scalar.activation(h2[t][:, v0 : v0 + w], bank[:], ACT.Copy, scale=0.0625)
+                banks.append(bank)
+            for t in range(PACK):
+                nc.scalar.activation(h2_again[:, t, v0 : v0 + w], banks[t][:], ACT.Copy, scale=0.0625)
+
+        out_rows = out_0.rearrange("(p t) v -> p t v", t=PACK)
+        out_words = out_1[0].rearrange("p v j -> p (v j)").bitcast(I32)
+        y_scales = sb([P, V], U8, "y_scales")
+        for c, (v0, w) in enumerate(spans(OUT_CHUNKS)):
+            entries = slice(v0 // 16, (v0 + w) // 16)
+            gate = sb([P, PACK, w], F32, f"gate{c}")
+            pull = sb([P, PACK, w], F32, f"pull{c}")
+            for t in range(PACK):
+                nc.scalar.activation(gate[:, t, :], h2[t][:].indirect(n2_sb[:, entries]), ACT.Sigmoid)
+                nc.vector.tensor_tensor(
+                    pull[:, t, :], h2[t][:].indirect(n3_sb[:, entries]), h2_again[:, t, v0 : v0 + w], ALU.subtract
+                )
+            gated = sb([P, PACK, w], F32, f"gated{c}")
+            nc.vector.tensor_tensor(gated[:], pull[:], gate[:], ALU.mult)
+            y = sb([P, PACK, w], F32, f"y{c}")
+            nc.vector.tensor_tensor(y[:], gated[:], h2_again[:, :, v0 : v0 + w], ALU.add)
+            nc.sync.dma_start(out_rows[:, :, v0 : v0 + w], y[:])
+            y_bf = sb([P, PACK * w], BF16, f"y_bf{c}")
+            nc.scalar.copy(y_bf[:].rearrange("p (v t) -> p v t", t=PACK), y[:].rearrange("p t v -> p v t"))
+            y_words = sb([P, w], U32, f"y_words{c}")
+            nc.vector.quantize_mx(out=y_words[:].bitcast(FP8X4), scales=y_scales[:, v0 : v0 + w], in_=y_bf[:])
+            nc.sync.dma_start(out_words[:, v0 : v0 + w], y_words[:].bitcast(I32))
+        for q in range(4):
+            queue = nc.scalar if q % 2 else nc.sync
+            queue.dma_start(out_2[0][4 * q : 4 * q + 4, :].bitcast(I32), y_scales[32 * q : 32 * q + 4, :].bitcast(I32))

@@ -33,8 +33,14 @@ def tile_picked_ringpgaptrack_none_po_kernel(
         keep = ctx.enter_context(tc.tile_pool(name="keep", bufs=1))
         psum = ctx.enter_context(tc.psum_pool(name="psum", bufs=1))
 
-        def sb(shape, dtype, name):
-            return keep.tile(shape, dtype, name=name, align_bytes=64)
+        def sb(shape, dtype, name, tag=None, bufs=1):
+            return keep.tile(shape, dtype, name=name, tag=tag or name, bufs=bufs, align_bytes=64)
+
+        def weave(copy, packed, rows):
+            copy(
+                packed.rearrange("p (c i t) -> p c t i", t=PACK, i=4),
+                rows.rearrange("p t (c i) -> p c t i", i=4),
+            )
 
         offs_sb = sb([P, S // 16], U16, "offs_sb")
         k1_sb = sb([P, H // 16], U16, "k1_sb")
@@ -45,24 +51,23 @@ def tile_picked_ringpgaptrack_none_po_kernel(
         dw_all = sb([P, G], I32, "dw_all")
         xs_all = sb([P, T], U8, "xs_all")
         ds_all = sb([P, G], U8, "ds_all")
-        ds_plane = sb([P, H], U8, "ds_plane")
+        planes = sb([P, H + S], U8, "planes")
         gs_sb = sb([P, PACK], F32, "gs_sb")
 
         nc.vector.memset(ds_all[:].bitcast(I32), 0)
-        nc.vector.memset(xs_all[:].bitcast(I32), 0)
-        nc.vector.memset(ds_plane[:].bitcast(I32), 0)
+        nc.gpsimd.memset(xs_all[:].bitcast(I32), 0)
+        nc.gpsimd.memset(planes[:].bitcast(I32), 0)
 
         nc.sync.dma_start(k1_sb[:], k1)
+        nc.scalar.dma_start(gs_sb[:], gs.rearrange("(p t) o -> p (t o)", t=PACK))
+        nc.sync.dma_start(ds_all[0:P:8, :].bitcast(I32), d_scales[0].bitcast(I32))
         nc.sync.dma_start(offs_sb[:], offs)
-        nc.sync.dma_start(n1_sb[:], n1)
-        nc.scalar.dma_start(ds_all[0:P:8, :].bitcast(I32), d_scales[0].bitcast(I32))
+        nc.sync.dma_start(xs_all[0:P:8, :].bitcast(I32), x_scales[0].bitcast(I32))
         nc.sync.dma_start(dw_all[:], d_words[0].rearrange("p n j -> p (n j)").bitcast(I32))
         nc.sync.dma_start(xw_all[:], x_words[0].rearrange("p n j -> p (n j)").bitcast(I32))
+        nc.sync.dma_start(n1_sb[:], n1)
         nc.sync.dma_start(n2_sb[:], n2)
         nc.sync.dma_start(n3_sb[:], n3)
-        for q in range(4):
-            nc.gpsimd.dma_start(xs_all[32 * q : 32 * q + 4, :].bitcast(I32), x_scales[0][4 * q : 4 * q + 4, :].bitcast(I32))
-        nc.gpsimd.dma_start(gs_sb[:], gs.rearrange("(p t) o -> p (t o)", t=PACK))
 
         warm = sb([P, 1], F32, "warm")
         nc.gpsimd.memset(warm[:], 0.0)
@@ -73,22 +78,21 @@ def tile_picked_ringpgaptrack_none_po_kernel(
         nc.scalar.activation(gs_64th[:], gs_sb[:], ACT.Copy, scale=1.0 / 64.0)
         nc.scalar.activation(gs_sign[:], gs_sb[:], ACT.Sign)
 
-        ds_picked = sb([P, H], U8, "ds_picked")
-        ds_dealt = sb([P, H], U8, "ds_dealt")
-        nc.vector.tensor_copy(ds_picked[:], ds_all[:].indirect(k1_sb[:]))
-        nc.vector.tensor_copy(
-            ds_dealt[:].rearrange("p (t m) -> p t m", t=PACK), ds_picked[:].rearrange("p (m t) -> p t m", t=PACK)
-        )
-        for q in range(4):
-            nc.sync.dma_start(
-                ds_plane[32 * q : 32 * q + 4, :].bitcast(I32), ds_dealt[32 * q : 32 * q + 32 : 8, :].bitcast(I32)
-            )
-
         half = S // 2
-        xs = [sb([P, half], U8, f"xs{u}") for u in range(2)]
-        xw = [sb([P, half], U32, f"xw{u}") for u in range(2)]
         half_lists = [offs_sb[:, u * half // 16 : (u + 1) * half // 16] for u in range(2)]
-        nc.vector.tensor_copy(xs[0][:], xs_all[:].indirect(half_lists[0]))
+        ds_picked = sb([P, H], U8, "ds_picked")
+        xs_picked = sb([P, S], U8, "xs_picked")
+        staged = sb([P, H + S], U8, "staged")
+        nc.vector.tensor_copy(ds_picked[:], ds_all[:].indirect(k1_sb[:]))
+        nc.vector.tensor_copy(xs_picked[:], xs_all[:].indirect(offs_sb[:]))
+        nc.vector.tensor_copy(
+            staged[:, 0:H].rearrange("p (t m) -> p t m", t=PACK), ds_picked[:].rearrange("p (m t) -> p t m", t=PACK)
+        )
+        nc.vector.tensor_copy(staged[:, H : H + S].bitcast(I32), xs_picked[:].bitcast(I32))
+        for q in range(4):
+            nc.scalar.dma_start(
+                planes[32 * q : 32 * q + 4, :].bitcast(I32), staged[32 * q : 32 * q + 32 : 8, :].bitcast(I32)
+            )
 
         dw_picked = sb([P, H], U32, "dw_picked")
         dw_dealt = sb([P, H], U32, "dw_dealt")
@@ -96,14 +100,16 @@ def tile_picked_ringpgaptrack_none_po_kernel(
         nc.vector.tensor_copy(
             dw_dealt[:].rearrange("p (t m) -> p t m", t=PACK), dw_picked[:].rearrange("p (m t) -> p t m", t=PACK)
         )
-        nc.vector.tensor_copy(xs[1][:], xs_all[:].indirect(half_lists[1]))
+        xw = [sb([P, half], U32, f"xw{u}") for u in range(2)]
+        for u in range(2):
+            nc.vector.tensor_copy(xw[u][:], xw_all[:].bitcast(U32).indirect(half_lists[u]))
 
         def product(bank, t, words, scales):
             cols = slice(t * P, (t + 1) * P)
             nc.tensor.matmul_mx(
                 out=bank,
                 lhsT=dw_dealt[:, cols].bitcast(FP8X4),
-                lhsT_scale=ds_plane[:, cols],
+                lhsT_scale=planes[:, cols],
                 rhs=words.bitcast(FP8X4),
                 rhs_scale=scales,
                 start=True,
@@ -111,21 +117,22 @@ def tile_picked_ringpgaptrack_none_po_kernel(
             )
 
         h = [sb([P, S], F32, f"h{t}") for t in range(PACK)]
-        h_banks = {}
-        for u in range(2):
-            nc.vector.tensor_copy(xw[u][:], xw_all[:].bitcast(U32).indirect(half_lists[u]))
-            for t in range(PACK):
-                h_banks[t, u] = psum.tile([P, half], F32, name=f"h_bank{t}{u}", tag=f"bank{PACK * u + t}")
-                product(h_banks[t, u][:], t, xw[u][:], xs[u][:])
-        for t, u in [(t, u) for t in range(PACK) for u in range(2)]:
-            nc.scalar.activation(
-                h[t][:, u * half : (u + 1) * half], h_banks[t, u][:], ACT.Copy, scale=gs_64th[:, t : t + 1]
-            )
+        for t in range(PACK):
+            for u in range(2):
+                bank = psum.tile([P, half], F32, name=f"h_bank{t}{u}", tag=f"bank{PACK * u + t}")
+                product(bank[:], t, xw[u][:], planes[:, H + u * half : H + (u + 1) * half])
+                nc.scalar.activation(h[t][:, u * half : (u + 1) * half], bank[:], ACT.Copy, scale=gs_64th[:, t : t + 1])
 
         h2 = [sb([P, V], F32, f"h2{t}") for t in range(PACK)]
         h2_again = sb([P, PACK, V], F32, "h2_again")
+
+        def second_copy(banks, v0, w):
+            for t in range(PACK):
+                nc.scalar.activation(h2_again[:, t, v0 : v0 + w], banks[t][:], ACT.Copy, scale=0.0625)
+
         for c, (v0, w) in enumerate(spans(Z_CHUNKS)):
-            lined = sb([P, PACK, 2 * w], F32, f"lined{c}")
+            last = c == len(Z_CHUNKS) - 1
+            lined = sb([P, PACK, 2 * w], F32, f"lined{c}", tag="lined", bufs=1)
             for t in range(PACK):
                 nc.vector.tensor_copy(lined[:, t, :], h[t][:].indirect(n1_sb[:, 2 * v0 // 16 : 2 * (v0 + w) // 16]))
             pairs = lined[:].rearrange("p t (v e) -> p (t v) e", e=2)
@@ -135,14 +142,14 @@ def tile_picked_ringpgaptrack_none_po_kernel(
             nc.vector.tensor_tensor(total[:], pairs[:, :, 0], pairs[:, :, 1], ALU.add)
             spread = sb([P, PACK * w], F32, f"spread{c}")
             nc.scalar.activation(spread[:], gap[:], ACT.Abs, scale=3.0)
-            z = sb([P, PACK * w], F32, f"z{c}")
+            z = sb([P, PACK, w], F32, f"z{c}")
             for t in range(PACK):
                 row = slice(t * w, (t + 1) * w)
                 nc.vector.scalar_tensor_tensor(
-                    z[:, row], spread[:, row], gs_sign[:, t : t + 1], total[:, row], ALU.mult, ALU.add
+                    z[:, t, :], spread[:, row], gs_sign[:, t : t + 1], total[:, row], ALU.mult, ALU.add
                 )
             z_bf = sb([P, PACK * w], BF16, f"z_bf{c}")
-            nc.scalar.copy(z_bf[:].rearrange("p (v t) -> p v t", t=PACK), z[:].rearrange("p (t v) -> p v t", t=PACK))
+            weave(nc.vector.tensor_copy if last else nc.scalar.copy, z_bf[:], z[:])
             z_words = sb([P, w], U32, f"z_words{c}")
             z_scales = sb([P, w], U8, f"z_scales{c}")
             nc.vector.quantize_mx(out=z_words[:].bitcast(FP8X4), scales=z_scales[:], in_=z_bf[:])
@@ -152,31 +159,51 @@ def tile_picked_ringpgaptrack_none_po_kernel(
                 product(bank[:], t, z_words[:], z_scales[:])
                 nc.scalar.activation(h2[t][:, v0 : v0 + w], bank[:], ACT.Copy, scale=0.0625)
                 banks.append(bank)
-            for t in range(PACK):
-                nc.scalar.activation(h2_again[:, t, v0 : v0 + w], banks[t][:], ACT.Copy, scale=0.0625)
+            if not last:
+                second_copy(banks, v0, w)
 
         out_rows = out_0.rearrange("(p t) v -> p t v", t=PACK)
         out_words = out_1[0].rearrange("p v j -> p (v j)").bitcast(I32)
         y_scales = sb([P, V], U8, "y_scales")
-        for c, (v0, w) in enumerate(spans(OUT_CHUNKS)):
+        chunks = spans(OUT_CHUNKS)
+        gate = [sb([P, PACK, w], F32, f"gate{c}") for c, (v0, w) in enumerate(chunks)]
+        pull = [sb([P, PACK, w], F32, f"pull{c}") for c, (v0, w) in enumerate(chunks)]
+        gated = [sb([P, PACK, w], F32, f"gated{c}") for c, (v0, w) in enumerate(chunks)]
+        y = [sb([P, PACK, w], F32, f"y{c}") for c, (v0, w) in enumerate(chunks)]
+        y_bfs = [sb([P, PACK * w], BF16, f"y_bf{c}") for c, (v0, w) in enumerate(chunks)]
+        y_words = [sb([P, w], U32, f"y_words{c}") for c, (v0, w) in enumerate(chunks)]
+
+        def fetch(c, rows):
+            if c >= len(chunks):
+                return
+            v0, w = chunks[c]
             entries = slice(v0 // 16, (v0 + w) // 16)
-            gate = sb([P, PACK, w], F32, f"gate{c}")
-            pull = sb([P, PACK, w], F32, f"pull{c}")
-            for t in range(PACK):
-                nc.scalar.activation(gate[:, t, :], h2[t][:].indirect(n2_sb[:, entries]), ACT.Sigmoid)
+            for t in rows:
+                nc.scalar.activation(gate[c][:, t, :], h2[t][:].indirect(n2_sb[:, entries]), ACT.Sigmoid)
                 nc.vector.tensor_tensor(
-                    pull[:, t, :], h2[t][:].indirect(n3_sb[:, entries]), h2_again[:, t, v0 : v0 + w], ALU.subtract
+                    pull[c][:, t, :], h2[t][:].indirect(n3_sb[:, entries]), h2_again[:, t, v0 : v0 + w], ALU.subtract
                 )
-            gated = sb([P, PACK, w], F32, f"gated{c}")
-            nc.vector.tensor_tensor(gated[:], pull[:], gate[:], ALU.mult)
-            y = sb([P, PACK, w], F32, f"y{c}")
-            nc.vector.tensor_tensor(y[:], gated[:], h2_again[:, :, v0 : v0 + w], ALU.add)
-            nc.sync.dma_start(out_rows[:, :, v0 : v0 + w], y[:])
-            y_bf = sb([P, PACK * w], BF16, f"y_bf{c}")
-            nc.scalar.copy(y_bf[:].rearrange("p (v t) -> p v t", t=PACK), y[:].rearrange("p t v -> p v t"))
-            y_words = sb([P, w], U32, f"y_words{c}")
-            nc.vector.quantize_mx(out=y_words[:].bitcast(FP8X4), scales=y_scales[:, v0 : v0 + w], in_=y_bf[:])
-            nc.sync.dma_start(out_words[:, v0 : v0 + w], y_words[:].bitcast(I32))
+
+        def quantise(c):
+            v0, w = chunks[c]
+            nc.vector.quantize_mx(out=y_words[c][:].bitcast(FP8X4), scales=y_scales[:, v0 : v0 + w], in_=y_bfs[c][:])
+            nc.sync.dma_start(out_words[:, v0 : v0 + w], y_words[c][:].bitcast(I32))
+
+        fetch(0, range(PACK))
+        second_copy(banks, *spans(Z_CHUNKS)[-1])
+        for c, (v0, w) in enumerate(chunks):
+            last = c == len(chunks) - 1
+            fetch(c + 1, range(0, 2))
+            nc.vector.tensor_tensor(gated[c][:], pull[c][:], gate[c][:], ALU.mult)
+            fetch(c + 1, range(2, PACK))
+            if last:
+                quantise(c - 1)
+            nc.vector.tensor_tensor(y[c][:], gated[c][:], h2_again[:, :, v0 : v0 + w], ALU.add)
+            nc.sync.dma_start(out_rows[:, :, v0 : v0 + w], y[c][:])
+            weave(nc.vector.tensor_copy if last else nc.scalar.copy, y_bfs[c][:], y[c][:])
+            if 0 < c < len(chunks) - 1:
+                quantise(c - 1)
+        quantise(len(chunks) - 1)
         for q in range(4):
-            queue = nc.scalar if q % 2 else nc.sync
+            queue = nc.scalar if q % 2 == 0 else nc.sync
             queue.dma_start(out_2[0][4 * q : 4 * q + 4, :].bitcast(I32), y_scales[32 * q : 32 * q + 4, :].bitcast(I32))

@@ -1,6 +1,7 @@
 from contextlib import ExitStack
 
 import concourse.mybir as mybir
+from concourse.masks import make_identity
 
 F32 = mybir.dt.float32
 BF16 = mybir.dt.bfloat16
@@ -14,15 +15,14 @@ ACT = mybir.ActivationFunctionType
 
 P = 128
 PACK = 4
-T, S, V, G, H = 2048, 1024, 512, 2048, 512
-FLOPS = 2 * 512 * H * (S + V)
-Z_CHUNKS = [256,128,128]
-OUT_CHUNKS = [256,128,128]
+GROUP = 16
+K, T, S, V, G, H = 512, 2048, 1024, 512, 2048, 512
+FLOPS = 2 * K * H * (S + V)
 
-
-def spans(widths):
-    starts = [sum(widths[:i]) for i in range(len(widths))]
-    return list(zip(starts, widths))
+X_HALF = S // 2
+Z_HALF = V // 2
+OUT_CHUNKS = [128,256,128]
+VECTOR_EMPTIES = 2
 
 
 def tile_picked_ringpgaptrack_none_po_kernel(
@@ -33,8 +33,14 @@ def tile_picked_ringpgaptrack_none_po_kernel(
         keep = ctx.enter_context(tc.tile_pool(name="keep", bufs=1))
         psum = ctx.enter_context(tc.psum_pool(name="psum", bufs=1))
 
-        def sb(shape, dtype, name, tag=None, bufs=1):
-            return keep.tile(shape, dtype, name=name, tag=tag or name, bufs=bufs, align_bytes=64)
+        def sbuf(shape, dtype, name):
+            return keep.tile(shape, dtype, name=name, align_bytes=64)
+
+        def bank(width, name, side, t):
+            return psum.tile([P, width], F32, name=name, tag=f"bank{side}{t}")
+
+        def entries(list_tile, first, count):
+            return list_tile[:, first // GROUP : (first + count) // GROUP]
 
         def weave(copy, packed, rows):
             copy(
@@ -42,73 +48,78 @@ def tile_picked_ringpgaptrack_none_po_kernel(
                 rows.rearrange("p t (c i) -> p c t i", i=4),
             )
 
-        offs_sb = sb([P, S // 16], U16, "offs_sb")
-        k1_sb = sb([P, H // 16], U16, "k1_sb")
-        n1_sb = sb([P, S // 16], U16, "n1_sb")
-        n2_sb = sb([P, V // 16], U16, "n2_sb")
-        n3_sb = sb([P, V // 16], U16, "n3_sb")
-        xw_all = sb([P, T], I32, "xw_all")
-        dw_all = sb([P, G], I32, "dw_all")
-        xs_all = sb([P, T], U8, "xs_all")
-        ds_all = sb([P, G], U8, "ds_all")
-        planes = sb([P, H + S], U8, "planes")
-        gs_sb = sb([P, PACK], F32, "gs_sb")
+        def deal(dealt, picked):
+            nc.vector.tensor_copy(
+                dealt.rearrange("p (t m) -> p t m", t=PACK), picked.rearrange("p (m t) -> p t m", t=PACK)
+            )
 
-        nc.vector.memset(ds_all[:].bitcast(I32), 0)
-        nc.gpsimd.memset(xs_all[:].bitcast(I32), 0)
+        offs_sb = sbuf([P, S // GROUP], U16, "offs_sb")
+        k1_sb = sbuf([P, H // GROUP], U16, "k1_sb")
+        n1_sb = sbuf([P, S // GROUP], U16, "n1_sb")
+        n2_sb = sbuf([P, V // GROUP], U16, "n2_sb")
+        n3_sb = sbuf([P, V // GROUP], U16, "n3_sb")
+        x_words_sb = sbuf([P, T], I32, "x_words_sb")
+        d_words_sb = sbuf([P, G], I32, "d_words_sb")
+        x_scales_sb = sbuf([P, T], U8, "x_scales_sb")
+        d_scales_sb = sbuf([P, G], U8, "d_scales_sb")
+        planes = sbuf([P, H + S], U8, "planes")
+        gs_sb = sbuf([P, PACK], F32, "gs_sb")
+
+        nc.vector.memset(d_scales_sb[:, 0 : G // 2].bitcast(I32), 0)
+        nc.gpsimd.memset(d_scales_sb[:, G // 2 : G].bitcast(I32), 0)
+        nc.gpsimd.memset(x_scales_sb[:].bitcast(I32), 0)
         nc.gpsimd.memset(planes[:].bitcast(I32), 0)
 
         nc.sync.dma_start(k1_sb[:], k1)
         nc.scalar.dma_start(gs_sb[:], gs.rearrange("(p t) o -> p (t o)", t=PACK))
-        nc.sync.dma_start(ds_all[0:P:8, :].bitcast(I32), d_scales[0].bitcast(I32))
+        nc.sync.dma_start(d_scales_sb[0:P:8, :].bitcast(I32), d_scales[0].bitcast(I32))
         nc.sync.dma_start(offs_sb[:], offs)
-        nc.sync.dma_start(xs_all[0:P:8, :].bitcast(I32), x_scales[0].bitcast(I32))
-        nc.sync.dma_start(dw_all[:], d_words[0].rearrange("p n j -> p (n j)").bitcast(I32))
-        nc.sync.dma_start(xw_all[:], x_words[0].rearrange("p n j -> p (n j)").bitcast(I32))
+        nc.sync.dma_start(x_scales_sb[0:P:8, :].bitcast(I32), x_scales[0].bitcast(I32))
+        nc.sync.dma_start(d_words_sb[:], d_words[0].rearrange("p n j -> p (n j)").bitcast(I32))
+        nc.sync.dma_start(x_words_sb[:], x_words[0].rearrange("p n j -> p (n j)").bitcast(I32))
         nc.sync.dma_start(n1_sb[:], n1)
         nc.sync.dma_start(n2_sb[:], n2)
         nc.sync.dma_start(n3_sb[:], n3)
 
-        warm = sb([P, 1], F32, "warm")
+        warm = sbuf([P, 1], F32, "warm")
         nc.gpsimd.memset(warm[:], 0.0)
         nc.scalar.activation(warm[:], warm[:], ACT.Sigmoid)
 
-        gs_64th = sb([P, PACK], F32, "gs_64th")
-        gs_sign = sb([P, PACK], F32, "gs_sign")
+        identity = sbuf([P, P], F32, "identity")
+        make_identity(nc, identity[:])
+
+        gs_64th = sbuf([P, PACK], F32, "gs_64th")
+        gs_sign = sbuf([P, PACK], F32, "gs_sign")
         nc.scalar.activation(gs_64th[:], gs_sb[:], ACT.Copy, scale=1.0 / 64.0)
         nc.scalar.activation(gs_sign[:], gs_sb[:], ACT.Sign)
 
-        half = S // 2
-        half_lists = [offs_sb[:, u * half // 16 : (u + 1) * half // 16] for u in range(2)]
-        ds_picked = sb([P, H], U8, "ds_picked")
-        xs_picked = sb([P, S], U8, "xs_picked")
-        staged = sb([P, H + S], U8, "staged")
-        nc.vector.tensor_copy(ds_picked[:], ds_all[:].indirect(k1_sb[:]))
-        nc.vector.tensor_copy(xs_picked[:], xs_all[:].indirect(offs_sb[:]))
-        nc.vector.tensor_copy(
-            staged[:, 0:H].rearrange("p (t m) -> p t m", t=PACK), ds_picked[:].rearrange("p (m t) -> p t m", t=PACK)
-        )
-        nc.vector.tensor_copy(staged[:, H : H + S].bitcast(I32), xs_picked[:].bitcast(I32))
+        d_scales_picked = sbuf([P, H], U8, "d_scales_picked")
+        x_scales_picked = sbuf([P, S], U8, "x_scales_picked")
+        staged = sbuf([P, H + S], U8, "staged")
+        nc.vector.tensor_copy(d_scales_picked[:], d_scales_sb[:].indirect(k1_sb[:]))
+        nc.vector.tensor_copy(x_scales_picked[:], x_scales_sb[:].indirect(offs_sb[:]))
+        deal(staged[:, 0:H], d_scales_picked[:])
+        nc.vector.tensor_copy(staged[:, H : H + S].bitcast(I32), x_scales_picked[:].bitcast(I32))
         for q in range(4):
             nc.scalar.dma_start(
                 planes[32 * q : 32 * q + 4, :].bitcast(I32), staged[32 * q : 32 * q + 32 : 8, :].bitcast(I32)
             )
 
-        dw_picked = sb([P, H], U32, "dw_picked")
-        dw_dealt = sb([P, H], U32, "dw_dealt")
-        nc.vector.tensor_copy(dw_picked[:], dw_all[:].bitcast(U32).indirect(k1_sb[:]))
-        nc.vector.tensor_copy(
-            dw_dealt[:].rearrange("p (t m) -> p t m", t=PACK), dw_picked[:].rearrange("p (m t) -> p t m", t=PACK)
-        )
-        xw = [sb([P, half], U32, f"xw{u}") for u in range(2)]
+        d_picked = sbuf([P, H], U32, "d_picked")
+        d_dealt = sbuf([P, H], U32, "d_dealt")
+        nc.vector.tensor_copy(d_picked[:], d_words_sb[:].bitcast(U32).indirect(k1_sb[:]))
+        deal(d_dealt[:], d_picked[:])
+        x_picked = [sbuf([P, X_HALF], U32, f"x_picked{u}") for u in range(2)]
         for u in range(2):
-            nc.vector.tensor_copy(xw[u][:], xw_all[:].bitcast(U32).indirect(half_lists[u]))
+            nc.vector.tensor_copy(
+                x_picked[u][:], x_words_sb[:].bitcast(U32).indirect(entries(offs_sb, u * X_HALF, X_HALF))
+            )
 
-        def product(bank, t, words, scales):
+        def product(out, t, words, scales):
             cols = slice(t * P, (t + 1) * P)
             nc.tensor.matmul_mx(
-                out=bank,
-                lhsT=dw_dealt[:, cols].bitcast(FP8X4),
+                out=out,
+                lhsT=d_dealt[:, cols].bitcast(FP8X4),
                 lhsT_scale=planes[:, cols],
                 rhs=words.bitcast(FP8X4),
                 rhs_scale=scales,
@@ -116,94 +127,114 @@ def tile_picked_ringpgaptrack_none_po_kernel(
                 stop=True,
             )
 
-        h = [sb([P, S], F32, f"h{t}") for t in range(PACK)]
+        h = [sbuf([P, S], F32, f"h{t}") for t in range(PACK)]
         for t in range(PACK):
             for u in range(2):
-                bank = psum.tile([P, half], F32, name=f"h_bank{t}{u}", tag=f"bank{PACK * u + t}")
-                product(bank[:], t, xw[u][:], planes[:, H + u * half : H + (u + 1) * half])
-                nc.scalar.activation(h[t][:, u * half : (u + 1) * half], bank[:], ACT.Copy, scale=gs_64th[:, t : t + 1])
-
-        h2 = [sb([P, V], F32, f"h2{t}") for t in range(PACK)]
-        h2_again = sb([P, PACK, V], F32, "h2_again")
-
-        def second_copy(banks, v0, w):
-            for t in range(PACK):
-                nc.scalar.activation(h2_again[:, t, v0 : v0 + w], banks[t][:], ACT.Copy, scale=0.0625)
-
-        for c, (v0, w) in enumerate(spans(Z_CHUNKS)):
-            last = c == len(Z_CHUNKS) - 1
-            lined = sb([P, PACK, 2 * w], F32, f"lined{c}", tag="lined", bufs=1)
-            for t in range(PACK):
-                nc.vector.tensor_copy(lined[:, t, :], h[t][:].indirect(n1_sb[:, 2 * v0 // 16 : 2 * (v0 + w) // 16]))
-            pairs = lined[:].rearrange("p t (v e) -> p (t v) e", e=2)
-            gap = sb([P, PACK * w], F32, f"gap{c}")
-            total = sb([P, PACK * w], F32, f"total{c}")
-            nc.vector.tensor_tensor(gap[:], pairs[:, :, 0], pairs[:, :, 1], ALU.subtract)
-            nc.vector.tensor_tensor(total[:], pairs[:, :, 0], pairs[:, :, 1], ALU.add)
-            spread = sb([P, PACK * w], F32, f"spread{c}")
-            nc.scalar.activation(spread[:], gap[:], ACT.Abs, scale=3.0)
-            z = sb([P, PACK, w], F32, f"z{c}")
-            for t in range(PACK):
-                row = slice(t * w, (t + 1) * w)
-                nc.vector.scalar_tensor_tensor(
-                    z[:, t, :], spread[:, row], gs_sign[:, t : t + 1], total[:, row], ALU.mult, ALU.add
+                sums = bank(X_HALF, f"h_sums{t}{u}", u, t)
+                product(sums[:], t, x_picked[u][:], planes[:, H + u * X_HALF : H + (u + 1) * X_HALF])
+                nc.scalar.activation(
+                    h[t][:, u * X_HALF : (u + 1) * X_HALF], sums[:], ACT.Copy, scale=gs_64th[:, t : t + 1]
                 )
-            z_bf = sb([P, PACK * w], BF16, f"z_bf{c}")
-            weave(nc.vector.tensor_copy if last else nc.scalar.copy, z_bf[:], z[:])
-            z_words = sb([P, w], U32, f"z_words{c}")
-            z_scales = sb([P, w], U8, f"z_scales{c}")
-            nc.vector.quantize_mx(out=z_words[:].bitcast(FP8X4), scales=z_scales[:], in_=z_bf[:])
-            banks = []
-            for t in range(PACK):
-                bank = psum.tile([P, w], F32, name=f"h2_bank{c}{t}", tag=f"bank{PACK * (c % 2) + t}")
-                product(bank[:], t, z_words[:], z_scales[:])
-                nc.scalar.activation(h2[t][:, v0 : v0 + w], bank[:], ACT.Copy, scale=0.0625)
-                banks.append(bank)
-            if not last:
-                second_copy(banks, v0, w)
 
+        total, spread = {}, {}
+        for t in range(PACK):
+            totals = bank(V, f"totals{t}", 0, t)
+            for c in range(2):
+                lined = sbuf([P, 2 * Z_HALF], F32, f"lined{t}{c}")
+                nc.vector.tensor_copy(lined[:], h[t][:].indirect(entries(n1_sb, c * 2 * Z_HALF, 2 * Z_HALF)))
+                pairs = lined[:].rearrange("p (v e) -> p v e", e=2)
+                gap = sbuf([P, Z_HALF], F32, f"gap{t}{c}")
+                if (t, c) == (PACK - 1, 1):
+                    total[t, c] = sbuf([P, Z_HALF], F32, "last_total")[:]
+                    nc.vector.tensor_tensor(gap[:], pairs[:, :, 0], pairs[:, :, 1], ALU.subtract)
+                    nc.vector.tensor_tensor(total[t, c], pairs[:, :, 0], pairs[:, :, 1], ALU.add)
+                else:
+                    nc.gpsimd.tensor_tensor(gap[:], pairs[:, :, 0], pairs[:, :, 1], ALU.subtract)
+                    blocks = [slice(j, j + P) for j in range(0, Z_HALF, P)]
+                    turned = bank(Z_HALF, f"turned{t}{c}", 1, t)
+                    for block in blocks:
+                        for e in range(2):
+                            nc.tensor.matmul(
+                                turned[:, block],
+                                pairs[:, block, e],
+                                identity[:],
+                                is_transpose=True,
+                                start=e == 0,
+                                stop=e == 1,
+                            )
+                    turned_sb = sbuf([P, Z_HALF], F32, f"turned_sb{t}{c}")
+                    nc.scalar.copy(turned_sb[:], turned[:])
+                    total[t, c] = totals[:, c * Z_HALF : (c + 1) * Z_HALF]
+                    for block in blocks:
+                        nc.tensor.transpose(total[t, c][:, block], turned_sb[:, block], identity[:])
+                spread[t, c] = sbuf([P, Z_HALF], F32, f"spread{t}{c}")
+                nc.scalar.activation(spread[t, c][:], gap[:], ACT.Abs, scale=3.0)
+
+        z_words, z_scales = [], []
+        for c, copy in enumerate((nc.scalar.copy, nc.vector.tensor_copy)):
+            z = sbuf([P, PACK, Z_HALF], F32, f"z{c}")
+            for t in range(PACK):
+                nc.vector.scalar_tensor_tensor(
+                    z[:, t, :], spread[t, c][:], gs_sign[:, t : t + 1], total[t, c], ALU.mult, ALU.add
+                )
+            z_packed = sbuf([P, PACK * Z_HALF], BF16, f"z_packed{c}")
+            weave(copy, z_packed[:], z[:])
+            z_words.append(sbuf([P, Z_HALF], U32, f"z_words{c}"))
+            z_scales.append(sbuf([P, Z_HALF], U8, f"z_scales{c}"))
+            nc.vector.quantize_mx(out=z_words[c][:].bitcast(FP8X4), scales=z_scales[c][:], in_=z_packed[:])
+
+        h2 = [sbuf([P, V], F32, f"h2{t}") for t in range(PACK)]
+        chunks = [slice(sum(OUT_CHUNKS[:c]), sum(OUT_CHUNKS[: c + 1])) for c in range(len(OUT_CHUNKS))]
+        gate = [sbuf([P, PACK, w], F32, f"gate{c}") for c, w in enumerate(OUT_CHUNKS)]
+        pulled = [sbuf([P, PACK, w], F32, f"pulled{c}") for c, w in enumerate(OUT_CHUNKS)]
+        dropped = [sbuf([P, PACK, w], F32, f"dropped{c}") for c, w in enumerate(OUT_CHUNKS)]
+        y_packed = [sbuf([P, PACK * w], BF16, f"y_packed{c}") for c, w in enumerate(OUT_CHUNKS)]
+        y_scales = sbuf([P, V], U8, "y_scales")
         out_rows = out_0.rearrange("(p t) v -> p t v", t=PACK)
         out_words = out_1[0].rearrange("p v j -> p (v j)").bitcast(I32)
-        y_scales = sb([P, V], U8, "y_scales")
-        chunks = spans(OUT_CHUNKS)
-        gate = [sb([P, PACK, w], F32, f"gate{c}") for c, (v0, w) in enumerate(chunks)]
-        pull = [sb([P, PACK, w], F32, f"pull{c}") for c, (v0, w) in enumerate(chunks)]
-        gated = [sb([P, PACK, w], F32, f"gated{c}") for c, (v0, w) in enumerate(chunks)]
-        y = [sb([P, PACK, w], F32, f"y{c}") for c, (v0, w) in enumerate(chunks)]
-        y_bfs = [sb([P, PACK * w], BF16, f"y_bf{c}") for c, (v0, w) in enumerate(chunks)]
-        y_words = [sb([P, w], U32, f"y_words{c}") for c, (v0, w) in enumerate(chunks)]
 
-        def fetch(c, rows):
-            if c >= len(chunks):
-                return
-            v0, w = chunks[c]
-            entries = slice(v0 // 16, (v0 + w) // 16)
-            for t in rows:
-                nc.scalar.activation(gate[c][:, t, :], h2[t][:].indirect(n2_sb[:, entries]), ACT.Sigmoid)
-                nc.vector.tensor_tensor(
-                    pull[c][:, t, :], h2[t][:].indirect(n3_sb[:, entries]), h2_again[:, t, v0 : v0 + w], ALU.subtract
-                )
+        def fetch(c, t):
+            first, width = chunks[c].start, OUT_CHUNKS[c]
+            nc.scalar.activation(gate[c][:, t, :], h2[t][:].indirect(entries(n2_sb, first, width)), ACT.Sigmoid)
+            nc.vector.tensor_tensor(
+                pulled[c][:, t, :], h2[t][:].indirect(entries(n3_sb, first, width)), gate[c][:, t, :], ALU.mult
+            )
+            nc.vector.scalar_tensor_tensor(
+                dropped[c][:, t, :], gate[c][:, t, :], 1.0, h2[t][:, chunks[c]], ALU.subtract, ALU.mult
+            )
+
+        def finish(c, copy):
+            y = sbuf([P, PACK, OUT_CHUNKS[c]], F32, f"y{c}")
+            nc.vector.tensor_tensor(y[:], pulled[c][:], dropped[c][:], ALU.subtract)
+            nc.sync.dma_start(out_rows[:, :, chunks[c]], y[:])
+            weave(copy, y_packed[c][:], y[:])
 
         def quantise(c):
-            v0, w = chunks[c]
-            nc.vector.quantize_mx(out=y_words[c][:].bitcast(FP8X4), scales=y_scales[:, v0 : v0 + w], in_=y_bfs[c][:])
-            nc.sync.dma_start(out_words[:, v0 : v0 + w], y_words[c][:].bitcast(I32))
+            y_words = sbuf([P, OUT_CHUNKS[c]], U32, f"y_words{c}")
+            nc.vector.quantize_mx(out=y_words[:].bitcast(FP8X4), scales=y_scales[:, chunks[c]], in_=y_packed[c][:])
+            nc.sync.dma_start(out_words[:, chunks[c]], y_words[:].bitcast(I32))
 
-        fetch(0, range(PACK))
-        second_copy(banks, *spans(Z_CHUNKS)[-1])
-        for c, (v0, w) in enumerate(chunks):
-            last = c == len(chunks) - 1
-            fetch(c + 1, range(0, 2))
-            nc.vector.tensor_tensor(gated[c][:], pull[c][:], gate[c][:], ALU.mult)
-            fetch(c + 1, range(2, PACK))
-            if last:
-                quantise(c - 1)
-            nc.vector.tensor_tensor(y[c][:], gated[c][:], h2_again[:, :, v0 : v0 + w], ALU.add)
-            nc.sync.dma_start(out_rows[:, :, v0 : v0 + w], y[c][:])
-            weave(nc.vector.tensor_copy if last else nc.scalar.copy, y_bfs[c][:], y[c][:])
-            if 0 < c < len(chunks) - 1:
-                quantise(c - 1)
-        quantise(len(chunks) - 1)
+        for t in range(PACK):
+            for c in range(2):
+                cols = slice(c * Z_HALF, (c + 1) * Z_HALF)
+                sums = bank(Z_HALF, f"h2_sums{t}{c}", 1 - c, t)
+                product(sums[:], t, z_words[c][:], z_scales[c][:])
+                if c == 1 and t < VECTOR_EMPTIES:
+                    nc.vector.tensor_scalar_mul(h2[t][:, cols], sums[:], 0.0625)
+                else:
+                    nc.scalar.activation(h2[t][:, cols], sums[:], ACT.Copy, scale=0.0625)
+            fetch(0, t)
+
+        last = len(OUT_CHUNKS) - 1
+        for c in range(last):
+            fetch(c + 1, 0)
+            finish(c, nc.scalar.copy)
+            for t in range(1, PACK):
+                fetch(c + 1, t)
+            quantise(c)
+        finish(last, nc.vector.tensor_copy)
+        quantise(last)
+
         for q in range(4):
             queue = nc.scalar if q % 2 == 0 else nc.sync
             queue.dma_start(out_2[0][4 * q : 4 * q + 4, :].bitcast(I32), y_scales[32 * q : 32 * q + 4, :].bitcast(I32))

from contextlib import ExitStack

import concourse.mybir as mybir
from concourse.masks import make_identity

F32 = mybir.dt.float32
BF16 = mybir.dt.bfloat16
I32 = mybir.dt.int32
U32 = mybir.dt.uint32
U16 = mybir.dt.uint16
U8 = mybir.dt.uint8
FP8X4 = mybir.dt.float8_e4m3fn_x4
ALU = mybir.AluOpType
ACT = mybir.ActivationFunctionType

P = 128
PACK = 4
GROUP = 16
K, T, S, V, G, H = 512, 2048, 1024, 512, 2048, 512
FLOPS = 2 * K * H * (S + V)

X_HALF = S // 2
Z_HALF = V // 2
OUT_CHUNKS = [128,256,128]
VECTOR_EMPTIES = 2


def tile_picked_ringpgaptrack_none_po_kernel(
    tc, x_words, x_scales, d_words, d_scales, gs, offs, k1, n1, n2, n3, out_0, out_1, out_2
):
    nc = tc.nc
    with ExitStack() as ctx:
        keep = ctx.enter_context(tc.tile_pool(name="keep", bufs=1))
        psum = ctx.enter_context(tc.psum_pool(name="psum", bufs=1))

        def sbuf(shape, dtype, name):
            return keep.tile(shape, dtype, name=name, align_bytes=64)

        def bank(width, name, side, t):
            return psum.tile([P, width], F32, name=name, tag=f"bank{side}{t}")

        def entries(list_tile, first, count):
            return list_tile[:, first // GROUP : (first + count) // GROUP]

        def weave(copy, packed, rows):
            copy(
                packed.rearrange("p (c i t) -> p c t i", t=PACK, i=4),
                rows.rearrange("p t (c i) -> p c t i", i=4),
            )

        def deal(dealt, picked):
            nc.vector.tensor_copy(
                dealt.rearrange("p (t m) -> p t m", t=PACK), picked.rearrange("p (m t) -> p t m", t=PACK)
            )

        offs_sb = sbuf([P, S // GROUP], U16, "offs_sb")
        k1_sb = sbuf([P, H // GROUP], U16, "k1_sb")
        n1_sb = sbuf([P, S // GROUP], U16, "n1_sb")
        n2_sb = sbuf([P, V // GROUP], U16, "n2_sb")
        n3_sb = sbuf([P, V // GROUP], U16, "n3_sb")
        x_words_sb = sbuf([P, T], I32, "x_words_sb")
        d_words_sb = sbuf([P, G], I32, "d_words_sb")
        x_scales_sb = sbuf([P, T], U8, "x_scales_sb")
        d_scales_sb = sbuf([P, G], U8, "d_scales_sb")
        planes = sbuf([P, H + S], U8, "planes")
        gs_sb = sbuf([P, PACK], F32, "gs_sb")

        nc.vector.memset(d_scales_sb[:, 0 : G // 2].bitcast(I32), 0)
        nc.gpsimd.memset(d_scales_sb[:, G // 2 : G].bitcast(I32), 0)
        nc.gpsimd.memset(x_scales_sb[:].bitcast(I32), 0)
        nc.gpsimd.memset(planes[:].bitcast(I32), 0)

        nc.sync.dma_start(k1_sb[:], k1)
        nc.scalar.dma_start(gs_sb[:], gs.rearrange("(p t) o -> p (t o)", t=PACK))
        nc.sync.dma_start(d_scales_sb[0:P:8, :].bitcast(I32), d_scales[0].bitcast(I32))
        nc.sync.dma_start(offs_sb[:], offs)
        nc.sync.dma_start(x_scales_sb[0:P:8, :].bitcast(I32), x_scales[0].bitcast(I32))
        nc.sync.dma_start(d_words_sb[:], d_words[0].rearrange("p n j -> p (n j)").bitcast(I32))
        nc.sync.dma_start(x_words_sb[:], x_words[0].rearrange("p n j -> p (n j)").bitcast(I32))
        nc.sync.dma_start(n1_sb[:], n1)
        nc.sync.dma_start(n2_sb[:], n2)
        nc.sync.dma_start(n3_sb[:], n3)

        warm = sbuf([P, 1], F32, "warm")
        nc.gpsimd.memset(warm[:], 0.0)
        nc.scalar.activation(warm[:], warm[:], ACT.Sigmoid)

        identity = sbuf([P, P], F32, "identity")
        make_identity(nc, identity[:])

        gs_64th = sbuf([P, PACK], F32, "gs_64th")
        gs_sign = sbuf([P, PACK], F32, "gs_sign")
        nc.scalar.activation(gs_64th[:], gs_sb[:], ACT.Copy, scale=1.0 / 64.0)
        nc.scalar.activation(gs_sign[:], gs_sb[:], ACT.Sign)

        d_scales_picked = sbuf([P, H], U8, "d_scales_picked")
        x_scales_picked = sbuf([P, S], U8, "x_scales_picked")
        staged = sbuf([P, H + S], U8, "staged")
        nc.vector.tensor_copy(d_scales_picked[:], d_scales_sb[:].indirect(k1_sb[:]))
        nc.vector.tensor_copy(x_scales_picked[:], x_scales_sb[:].indirect(offs_sb[:]))
        deal(staged[:, 0:H], d_scales_picked[:])
        nc.vector.tensor_copy(staged[:, H : H + S].bitcast(I32), x_scales_picked[:].bitcast(I32))
        for q in range(4):
            nc.scalar.dma_start(
                planes[32 * q : 32 * q + 4, :].bitcast(I32), staged[32 * q : 32 * q + 32 : 8, :].bitcast(I32)
            )

        d_picked = sbuf([P, H], U32, "d_picked")
        d_dealt = sbuf([P, H], U32, "d_dealt")
        nc.vector.tensor_copy(d_picked[:], d_words_sb[:].bitcast(U32).indirect(k1_sb[:]))
        deal(d_dealt[:], d_picked[:])
        x_picked = [sbuf([P, X_HALF], U32, f"x_picked{u}") for u in range(2)]
        for u in range(2):
            nc.vector.tensor_copy(
                x_picked[u][:], x_words_sb[:].bitcast(U32).indirect(entries(offs_sb, u * X_HALF, X_HALF))
            )

        def product(out, t, words, scales):
            cols = slice(t * P, (t + 1) * P)
            nc.tensor.matmul_mx(
                out=out,
                lhsT=d_dealt[:, cols].bitcast(FP8X4),
                lhsT_scale=planes[:, cols],
                rhs=words.bitcast(FP8X4),
                rhs_scale=scales,
                start=True,
                stop=True,
            )

        h = [sbuf([P, S], F32, f"h{t}") for t in range(PACK)]
        for t in range(PACK):
            for u in range(2):
                sums = bank(X_HALF, f"h_sums{t}{u}", u, t)
                product(sums[:], t, x_picked[u][:], planes[:, H + u * X_HALF : H + (u + 1) * X_HALF])
                nc.scalar.activation(
                    h[t][:, u * X_HALF : (u + 1) * X_HALF], sums[:], ACT.Copy, scale=gs_64th[:, t : t + 1]
                )

        total, spread = {}, {}
        for t in range(PACK):
            totals = bank(V, f"totals{t}", 0, t)
            for c in range(2):
                lined = sbuf([P, 2 * Z_HALF], F32, f"lined{t}{c}")
                nc.vector.tensor_copy(lined[:], h[t][:].indirect(entries(n1_sb, c * 2 * Z_HALF, 2 * Z_HALF)))
                pairs = lined[:].rearrange("p (v e) -> p v e", e=2)
                gap = sbuf([P, Z_HALF], F32, f"gap{t}{c}")
                if (t, c) == (PACK - 1, 1):
                    total[t, c] = sbuf([P, Z_HALF], F32, "last_total")[:]
                    nc.vector.tensor_tensor(gap[:], pairs[:, :, 0], pairs[:, :, 1], ALU.subtract)
                    nc.vector.tensor_tensor(total[t, c], pairs[:, :, 0], pairs[:, :, 1], ALU.add)
                else:
                    nc.gpsimd.tensor_tensor(gap[:], pairs[:, :, 0], pairs[:, :, 1], ALU.subtract)
                    blocks = [slice(j, j + P) for j in range(0, Z_HALF, P)]
                    turned = bank(Z_HALF, f"turned{t}{c}", 1, t)
                    for block in blocks:
                        for e in range(2):
                            nc.tensor.matmul(
                                turned[:, block],
                                pairs[:, block, e],
                                identity[:],
                                is_transpose=True,
                                start=e == 0,
                                stop=e == 1,
                            )
                    turned_sb = sbuf([P, Z_HALF], F32, f"turned_sb{t}{c}")
                    nc.scalar.copy(turned_sb[:], turned[:])
                    total[t, c] = totals[:, c * Z_HALF : (c + 1) * Z_HALF]
                    for block in blocks:
                        nc.tensor.transpose(total[t, c][:, block], turned_sb[:, block], identity[:])
                spread[t, c] = sbuf([P, Z_HALF], F32, f"spread{t}{c}")
                nc.scalar.activation(spread[t, c][:], gap[:], ACT.Abs, scale=3.0)

        z_words, z_scales = [], []
        for c, copy in enumerate((nc.scalar.copy, nc.vector.tensor_copy)):
            z = sbuf([P, PACK, Z_HALF], F32, f"z{c}")
            for t in range(PACK):
                nc.vector.scalar_tensor_tensor(
                    z[:, t, :], spread[t, c][:], gs_sign[:, t : t + 1], total[t, c], ALU.mult, ALU.add
                )
            z_packed = sbuf([P, PACK * Z_HALF], BF16, f"z_packed{c}")
            weave(copy, z_packed[:], z[:])
            z_words.append(sbuf([P, Z_HALF], U32, f"z_words{c}"))
            z_scales.append(sbuf([P, Z_HALF], U8, f"z_scales{c}"))
            nc.vector.quantize_mx(out=z_words[c][:].bitcast(FP8X4), scales=z_scales[c][:], in_=z_packed[:])

        h2 = [sbuf([P, V], F32, f"h2{t}") for t in range(PACK)]
        chunks = [slice(sum(OUT_CHUNKS[:c]), sum(OUT_CHUNKS[: c + 1])) for c in range(len(OUT_CHUNKS))]
        gate = [sbuf([P, PACK, w], F32, f"gate{c}") for c, w in enumerate(OUT_CHUNKS)]
        pulled = [sbuf([P, PACK, w], F32, f"pulled{c}") for c, w in enumerate(OUT_CHUNKS)]
        dropped = [sbuf([P, PACK, w], F32, f"dropped{c}") for c, w in enumerate(OUT_CHUNKS)]
        y_packed = [sbuf([P, PACK * w], BF16, f"y_packed{c}") for c, w in enumerate(OUT_CHUNKS)]
        y_scales = sbuf([P, V], U8, "y_scales")
        out_rows = out_0.rearrange("(p t) v -> p t v", t=PACK)
        out_words = out_1[0].rearrange("p v j -> p (v j)").bitcast(I32)

        def fetch(c, t):
            first, width = chunks[c].start, OUT_CHUNKS[c]
            nc.scalar.activation(gate[c][:, t, :], h2[t][:].indirect(entries(n2_sb, first, width)), ACT.Sigmoid)
            nc.vector.tensor_tensor(
                pulled[c][:, t, :], h2[t][:].indirect(entries(n3_sb, first, width)), gate[c][:, t, :], ALU.mult
            )
            nc.vector.scalar_tensor_tensor(
                dropped[c][:, t, :], gate[c][:, t, :], 1.0, h2[t][:, chunks[c]], ALU.subtract, ALU.mult
            )

        def finish(c, copy):
            y = sbuf([P, PACK, OUT_CHUNKS[c]], F32, f"y{c}")
            nc.vector.tensor_tensor(y[:], pulled[c][:], dropped[c][:], ALU.subtract)
            nc.sync.dma_start(out_rows[:, :, chunks[c]], y[:])
            weave(copy, y_packed[c][:], y[:])

        def quantise(c):
            y_words = sbuf([P, OUT_CHUNKS[c]], U32, f"y_words{c}")
            nc.vector.quantize_mx(out=y_words[:].bitcast(FP8X4), scales=y_scales[:, chunks[c]], in_=y_packed[c][:])
            nc.sync.dma_start(out_words[:, chunks[c]], y_words[:].bitcast(I32))

        for t in range(PACK):
            for c in range(2):
                cols = slice(c * Z_HALF, (c + 1) * Z_HALF)
                sums = bank(Z_HALF, f"h2_sums{t}{c}", 1 - c, t)
                product(sums[:], t, z_words[c][:], z_scales[c][:])
                if c == 1 and t < VECTOR_EMPTIES:
                    nc.vector.tensor_scalar_mul(h2[t][:, cols], sums[:], 0.0625)
                else:
                    nc.scalar.activation(h2[t][:, cols], sums[:], ACT.Copy, scale=0.0625)
            fetch(0, t)

        last = len(OUT_CHUNKS) - 1
        for c in range(last):
            fetch(c + 1, 0)
            finish(c, nc.scalar.copy)
            for t in range(1, PACK):
                fetch(c + 1, t)
            quantise(c)
        finish(last, nc.vector.tensor_copy)
        quantise(last)

        for q in range(4):
            queue = nc.scalar if q % 2 == 0 else nc.sync
            queue.dma_start(out_2[0][4 * q : 4 * q + 4, :].bitcast(I32), y_scales[32 * q : 32 * q + 4, :].bitcast(I32))
